import numpy as np
import ml_dtypes


def mxq(x, axis, fmt="e4m3"):
    dtype, down = {"e4m3": (ml_dtypes.float8_e4m3fn, 7), "e5m2": (ml_dtypes.float8_e5m2, 14)}[fmt]
    v = np.moveaxis(np.asarray(x, np.float32).astype(ml_dtypes.bfloat16).astype(np.float64), axis, -1)
    blocks = v.reshape(v.shape[:-1] + (-1, 32))
    amax = np.abs(blocks).max(-1, keepdims=True)
    byte = np.maximum(np.where(amax > 0, np.frexp(amax)[1] - 1 + 127, 0) - down, 1)
    scale = np.exp2(byte - 127.0)
    codes = (blocks / scale).astype(np.float32).astype(dtype).astype(np.float64)
    return np.moveaxis((codes * scale).reshape(v.shape), -1, axis)


WIDE = False


def mx_kscale(k):
    if not WIDE:
        return np.ones(k)
    levels = np.array([24, -24, 12, -12, 0])
    if k % 512:
        return np.exp2(np.random.permutation(np.resize(levels, k // 32))).repeat(32)
    a = np.empty((k // 512, 16))
    for p in range(k // 512):
        a[p, :8] = np.random.permutation(np.resize(levels, 8))
        for g in range(8):
            far = levels[np.abs(levels - a[p, g]) >= 10]
            a[p, g + 8] = far[np.random.randint(len(far))]
    return np.exp2(a.ravel()).repeat(32)


def f64(x):
    return np.asarray(x).astype(np.float64)


def striped(idx):
    return np.tile(idx.reshape(-1, 16).T, (8, 1)).astype(np.uint16)


def unstriped(offs):
    return offs[:16].T.reshape(-1).astype(np.int64)


E2M1 = np.array([0.0, 0.5, 1.0, 1.5, 2.0, 3.0, 4.0, 6.0, -0.0, -0.5, -1.0, -1.5, -2.0, -3.0, -4.0, -6.0])


def pack_weight(w, fmt):
    k, n = w.shape
    w = f64(np.asarray(w, np.float32).astype(ml_dtypes.bfloat16)).reshape(k // 32, 32, n)
    amax = np.abs(w).max(1)
    if fmt == "e4m3":
        byte = np.frexp(amax)[1] - 1 + 127 - 7
    else:
        mant, ex = np.frexp(amax / 6.0)
        byte = np.where(mant > 0.5, ex, ex - 1) + 127
    byte = np.clip(np.where(amax > 0, byte, 1), 1, 254)
    scaled = (w * np.exp2(127.0 - byte)[:, None, :]).reshape(k, n).astype(np.float32)
    by_word = np.ascontiguousarray(scaled.reshape(k // 512, 128, 4, n).transpose(0, 1, 3, 2))
    if fmt == "e4m3":
        words = by_word.astype(ml_dtypes.float8_e4m3fn).view(np.uint8)
    else:
        c = by_word.astype(ml_dtypes.float4_e2m1fn).view(np.uint8) & 0xF
        words = (c[..., 0::2] | (c[..., 1::2] << 4)).reshape(k // 512, 128, 2 * n)
    return np.ascontiguousarray(words), np.ascontiguousarray(byte.astype(np.uint8).reshape(k // 512, 16, n))


def unpack_weight(words, scales, fmt):
    g, _, n = scales.shape
    words = np.ascontiguousarray(words).reshape(g, 128, n, -1)
    if fmt == "e4m3":
        vals = words.view(ml_dtypes.float8_e4m3fn).astype(np.float64)
    else:
        nib = np.empty((g, 128, n, 4), np.uint8)
        nib[..., 0::2] = words & 0xF
        nib[..., 1::2] = words >> 4
        vals = E2M1[nib]
    vals = vals * np.repeat(np.exp2(scales.astype(np.float64) - 127.0), 8, axis=1)[..., None]
    return vals.transpose(0, 1, 3, 2).reshape(g * 512, n)


def pack_table4(v):
    words, scales = pack_weight(v, "e2m1")
    g, t = words.shape[0] // 2, v.shape[1]
    return np.ascontiguousarray(words.reshape(g, 2, 128, t, 2).transpose(0, 2, 3, 1, 4).reshape(g, 128, t, 4)), scales


def unpack_table4(words, scales):
    g, _, t, _ = words.shape
    return unpack_weight(words.reshape(g, 128, t, 2, 2).transpose(0, 3, 1, 2, 4).reshape(2 * g, 128, 2 * t), scales, "e2m1")


K, R, M, T, N, J = 1024, 1024, 1024, 2048, 512, 1024


def setup_inputs():
    n = np.random.standard_normal
    u = mx_kscale(R)[:, None]
    s = mx_kscale(K)[:, None]
    w = n((K, R)) / np.sqrt(K) / s / u.T
    w4 = pack_weight(w, "e2m1")
    rest = w - unpack_weight(*w4, "e2m1")
    p_r8 = pack_weight(rest, "e4m3")
    p_tab = pack_table4(n((R, T)) * u)
    return {
        "x": (n((K, M)) * s).astype(np.float32),
        "w4_words": w4[0],
        "w4_scales": w4[1],
        "r8_words": p_r8[0],
        "r8_scales": p_r8[1],
        "tab_words": p_tab[0],
        "tab_scales": p_tab[1],
        "wv": (n((R, N)) / np.sqrt(R) / u).astype(np.float32),
        "offs": striped(np.random.permutation(T)[:J]),
    }


def reference(x, w4_words, w4_scales, r8_words, r8_scales, tab_words, tab_scales, wv, offs):
    idx = unstriped(offs)
    x_ = mxq(f64(x), 0, "e4m3")
    w4_ = unpack_weight(w4_words, w4_scales, "e2m1")
    r8_ = unpack_weight(r8_words, r8_scales, "e4m3")
    qa = w4_.T @ x_ + r8_.T @ x_
    qa_ = mxq(qa, 0, "e4m3")
    tab_ = unpack_table4(tab_words, tab_scales)[:, idx]
    sc = qa_.T @ tab_
    wv_ = mxq(f64(wv), 0, "e4m3")
    vv = wv_.T @ tab_
    return np.maximum(sc, 0.0) * 0.03125, vv

@@ -1,0 +1,334 @@
+from contextlib import ExitStack
+
+import concourse.mybir as mybir
+
+K, R, M, T, N, J = 1024, 1024, 1024, 2048, 512, 1024
+FLOPS = 2 * (2 * K * R * M + R * M * J + R * N * J)
+
+F32 = mybir.dt.float32
+BF16 = mybir.dt.bfloat16
+I32 = mybir.dt.int32
+U32 = mybir.dt.uint32
+U16 = mybir.dt.uint16
+U8 = mybir.dt.uint8
+FP8X4 = mybir.dt.float8_e4m3fn_x4
+FP4X4 = mybir.dt.float4_e2m1fn_x4
+ACT = mybir.ActivationFunctionType
+ALU = mybir.AluOpType
+
+P = 128
+PACK = 4
+BANK = 512
+SCORE_SCALE = 0.03125
+
+
+def tile_list_mlat_resid_relu_kernel(
+    tc, x, w4_words, w4_scales, r8_words, r8_scales, tab_words, tab_scales, wv, offs, out_0, out_1
+):
+    nc = tc.nc
+    with ExitStack() as ctx:
+        keep = ctx.enter_context(tc.tile_pool(name="keep", bufs=1))
+        weaving = ctx.enter_context(tc.tile_pool(name="weaving", bufs=3))
+        psum = ctx.enter_context(tc.psum_pool(name="psum", bufs=4))
+
+        def tile(name, shape, dtype):
+            return keep.tile(shape, dtype, name=name, align_bytes=64)
+
+        def copy(engine, out, in_):
+            if engine == "S":
+                nc.scalar.activation(out, in_, ACT.Copy)
+            else:
+                nc.vector.tensor_copy(out, in_)
+
+        def weave(engine, dst, src):
+            copy(
+                engine,
+                dst.rearrange("p (c i) t -> p c t i", i=4),
+                src.rearrange("p t (c i) -> p c t i", i=4),
+            )
+
+        def unweave(dst, src, ways, run):
+            nc.vector.tensor_copy(
+                dst.rearrange("p (t c i) -> p c t i", t=ways, i=run),
+                src.rearrange("p (c i t) -> p c t i", t=ways, i=run),
+            )
+
+        def quantise(codes, scales, woven):
+            nc.vector.quantize_mx(
+                out=codes.bitcast(FP8X4), scales=scales, in_=woven.rearrange("p m t -> p (m t)")
+            )
+
+        x_rows = x.rearrange("(a p t) m -> a p t m", a=2, t=PACK)
+        wv_rows = wv.rearrange("(a p t) n -> a p t n", a=2, t=PACK)
+
+        w4s_raw = tile("w4s_raw", [P, 2 * R // 4], I32)
+        r8s_raw = tile("r8s_raw", [P, R // 4], I32)
+        tabs_raw = tile("tabs_raw", [P, T // 4], I32)
+        tab_s1 = [tile("tab_s1_%d" % g, [P, BANK // 4], I32) for g in range(2)]
+        nc.gpsimd.memset(r8s_raw[:], 0)
+        nc.vector.memset(w4s_raw[:], 0)
+        nc.gpsimd.memset(tabs_raw[:], 0)
+        for g in range(2):
+            nc.vector.memset(tab_s1[g][:], 0)
+
+        x_raw = {}
+
+        def load_x(h, a, c0, c1):
+            raw = tile("x_raw_%d_%d_%d" % (h, a, c0), [P, PACK, c1 - c0], F32)
+            nc.sync.dma_start(raw[:], x_rows[a, :, :, BANK * h + c0 : BANK * h + c1])
+            x_raw[(h, a, c0)] = raw
+
+        w4_raw = [tile("w4_raw_%d" % a, [P, R // 2], I32) for a in range(2)]
+        r8_raw = {(a, b): tile("r8_raw_%d_%d" % (a, b), [P, BANK], I32) for a in range(2) for b in range(2)}
+
+        def load_w4(a):
+            nc.sync.dma_start(w4_raw[a][:], w4_words[a].bitcast(I32))
+
+        def load_r8(a, b):
+            words = r8_words[a].rearrange("p r i -> p (r i)").bitcast(I32)
+            nc.sync.dma_start(r8_raw[(a, b)][:], words[:, BANK * b : BANK * (b + 1)])
+
+        def load_stacked_scales(queue, raw, scales):
+            for q in range(4):
+                queue.dma_start(raw[32 * q : 32 * q + 8, :], scales.bitcast(I32)[:, 4 * q : 4 * q + 4, :])
+
+        def load_w4_scales():
+            for q in range(4):
+                nc.sync.dma_start(
+                    w4s_raw[32 * q : 32 * q + 4, :].rearrange("p (a r) -> p a r", a=2),
+                    w4_scales.bitcast(I32)[:, 4 * q : 4 * q + 4, :].rearrange("a q r -> q a r"),
+                )
+
+        offsets = keep.tile([P, J // 16], U16, name="offsets")
+        tab_raw = tile("tab_raw", [P, T], I32)
+
+        def load_table_scales():
+            nc.sync.dma_start(offsets[:], offs)
+            load_stacked_scales(nc.sync, tabs_raw, tab_scales)
+
+        def load_table():
+            nc.sync.dma_start(tab_raw[:], tab_words[0].rearrange("p t i -> p (t i)").bitcast(I32))
+
+        load_x(0, 0, 0, 256)
+        load_stacked_scales(nc.sync, r8s_raw, r8_scales)
+        load_r8(0, 0)
+        load_r8(0, 1)
+        load_x(0, 0, 256, 512)
+        load_w4_scales()
+        load_w4(0)
+        load_x(0, 1, 0, 512)
+        load_w4(1)
+        load_r8(1, 0)
+        load_r8(1, 1)
+        load_table_scales()
+        load_x(1, 0, 0, 512)
+        load_x(1, 1, 0, 512)
+        load_table()
+        wv_raw = [tile("wv_raw_%d" % a, [P, PACK, N], F32) for a in range(2)]
+
+        def load_wv():
+            for a in range(2):
+                nc.sync.dma_start(wv_raw[a][:], wv_rows[a])
+
+        x_woven = {}
+
+        def woven_tile():
+            return weaving.tile([P, BANK, PACK], BF16, name="woven", align_bytes=64)
+
+        x_codes = {(h, a): tile("x_codes_%d_%d" % (h, a), [P, BANK], U32) for h in range(2) for a in range(2)}
+        x_scales = {(h, a): tile("x_scales_%d_%d" % (h, a), [P, BANK], U8) for h in range(2) for a in range(2)}
+        w4 = [tile("w4_%d" % a, [P, 2 * R], U8) for a in range(2)]
+        w4s = [tile("w4s_%d" % a, [P, R], U8) for a in range(2)]
+        r8 = {(a, b): tile("r8_%d_%d" % (a, b), [P, BANK], I32) for a in range(2) for b in range(2)}
+        r8s = [tile("r8s_%d" % b, [P, BANK], U8) for b in range(2)]
+
+        def weave_x(engine, h, a, load0, c0, c1):
+            if (h, a) not in x_woven:
+                x_woven.setdefault((h, a), woven_tile())
+            weave(engine, x_woven[(h, a)][:, c0:c1, :], x_raw[(h, a, load0)][:, :, c0 - load0 : c1 - load0])
+
+        def quantise_x(h, a, c0, c1):
+            quantise(x_codes[(h, a)][:, c0:c1], x_scales[(h, a)][:, c0:c1], x_woven[(h, a)][:, c0:c1, :])
+
+        def order_w4_scales(a):
+            unweave(w4s[a][:], w4s_raw[:].bitcast(U8)[:, R * a : R * (a + 1)], PACK, 16)
+
+        def order_w4(a):
+            unweave(w4[a][:].bitcast(U16), w4_raw[a][:].bitcast(U16), PACK, 8)
+
+        def order_r8_scales(b):
+            unweave(r8s[b][:], r8s_raw[:].bitcast(U8)[:, BANK * b : BANK * (b + 1)], PACK, 16)
+
+        def order_r8(a, b):
+            unweave(r8[(a, b)][:], r8_raw[(a, b)][:], PACK, 4)
+
+        def query_pass(acc, tier, h, a, b, t, start, stop, m0=0, m1=BANK):
+            c0 = 256 * t + P * b
+            if tier == "w4":
+                words = w4[a][:, 2 * c0 : 2 * (c0 + P)].bitcast(FP4X4)
+                scales = w4s[a][:, c0 : c0 + P]
+            else:
+                words = r8[(a, b)][:, P * t : P * (t + 1)].bitcast(FP8X4)
+                scales = r8s[b][4 * a :, P * t : P * (t + 1)]
+            nc.tensor.matmul_mx(
+                out=acc[:, m0:m1], lhsT=words, lhsT_scale=scales,
+                rhs=x_codes[(h, a)][:, m0:m1].bitcast(FP8X4), rhs_scale=x_scales[(h, a)][:, m0:m1],
+                start=start, stop=stop,
+            )
+
+        qa_flat = {(h, b): tile("qa_flat_%d_%d" % (h, b), [P, PACK, BANK], BF16) for h in range(2) for b in range(2)}
+        qa_codes = {(h, b): tile("qa_codes_%d_%d" % (h, b), [P, BANK], U32) for h in range(2) for b in range(2)}
+        qa_scales = {(h, b): tile("qa_scales_%d_%d" % (h, b), [P, BANK], U8) for h in range(2) for b in range(2)}
+        slices = [(b, t) for b in range(2) for t in range(PACK)]
+
+        def bank(side):
+            return psum.tile([P, BANK], F32, name="bank_%d" % side)
+
+        def open_first_half():
+            accs = {(b, t): bank(b) for b, t in slices}
+            for m0 in (0, 256):
+                for b, t in slices:
+                    query_pass(accs[(b, t)], "r8", 0, 0, b, t, m0 == 0, False, m0, m0 + 256)
+            for b, t in slices:
+                query_pass(accs[(b, t)], "w4", 0, 0, b, t, False, False)
+            return accs
+
+        def open_second_half(b):
+            accs = {(b, t): bank(0) for t in range(PACK)}
+            for t in range(PACK):
+                query_pass(accs[(b, t)], "r8", 1, 0, b, t, True, False)
+                query_pass(accs[(b, t)], "w4", 1, 0, b, t, False, False)
+            return accs
+
+        def close_queries(h, accs):
+            for b, t in accs:
+                query_pass(accs[(b, t)], "w4", h, 1, b, t, False, False)
+                query_pass(accs[(b, t)], "r8", h, 1, b, t, False, True)
+                copy("S", qa_flat[(h, b)][:, t, :], accs[(b, t)][:])
+
+        def quantise_qa(h, b):
+            woven = woven_tile()
+            weave("V", woven[:], qa_flat[(h, b)][:])
+            quantise(qa_codes[(h, b)][:], qa_scales[(h, b)][:], woven[:])
+
+        picked = [tile("picked_%d" % g, [P, BANK], U32) for g in range(2)]
+        tab = [tile("tab_%d" % g, [P, 2 * 2 * BANK], U8) for g in range(2)]
+        tab_s0 = [tile("tab_s0_%d" % g, [P, BANK], U8) for g in range(2)]
+
+        def gather_scales(g):
+            nc.vector.tensor_copy(tab_s0[g][:], tabs_raw[:].bitcast(U8).indirect(offsets[:, 32 * g : 32 * (g + 1)]))
+
+        def shift_scales(g):
+            for p0, rows in ((0, 64), (64, 32), (96, 4)):
+                nc.sync.dma_start(tab_s1[g][p0 : p0 + rows, :], tab_s0[g][:].bitcast(I32)[p0 + 4 : p0 + 4 + rows, :])
+
+        def gather_words(g):
+            nc.vector.tensor_copy(picked[g][:], tab_raw[:].bitcast(U32).indirect(offsets[:, 32 * g : 32 * (g + 1)]))
+
+        def part_words(g):
+            unweave(tab[g][:].bitcast(U16), picked[g][:].bitcast(U16), 2, 8)
+
+        def table_product(codes, scales, c0, g, side):
+            acc = bank(side)
+            for a in range(2):
+                plane = tab_s0[g][:] if a == 0 else tab_s1[g][:].bitcast(U8)
+                nc.tensor.matmul_mx(
+                    out=acc[:], lhsT=codes[a][:, c0 : c0 + P].bitcast(FP8X4), lhsT_scale=scales[a][:, c0 : c0 + P],
+                    rhs=tab[g][:, 2 * BANK * a : 2 * BANK * (a + 1)].bitcast(FP4X4),
+                    rhs_scale=plane,
+                    start=(a == 0), stop=(a == 1),
+                )
+            return acc
+
+        def score_tile(engine, h, i, g, side, staged):
+            codes = [qa_codes[(h, b)] for b in range(2)]
+            scales = [qa_scales[(h, b)] for b in range(2)]
+            acc = table_product(codes, scales, P * i, g, side)
+            if engine == "S":
+                nc.scalar.activation(staged, acc[:], ACT.Relu, scale=SCORE_SCALE)
+            else:
+                nc.vector.tensor_scalar(staged, acc[:], 0.0, SCORE_SCALE, ALU.max, ALU.mult)
+
+        def early_scores(g, engines):
+            for i in range(4):
+                staged = tile("scores_0_%d_%d" % (i, g), [P, BANK], F32)
+                score_tile(engines[i], 0, i, g, 1, staged[:])
+                nc.sync.dma_start(out_0[P * i : P * (i + 1), BANK * g : BANK * (g + 1)], staged[:])
+
+        def late_scores(engines, fine):
+            for i in range(4):
+                rows = slice(BANK + P * i, BANK + P * (i + 1))
+                staged = tile("scores_1_%d" % i, [P, J], F32)
+                for g in range(2):
+                    cols = slice(BANK * g, BANK * (g + 1))
+                    score_tile(engines[2 * i + g], 1, i, g, g, staged[:, cols])
+                    if i >= fine:
+                        nc.sync.dma_start(out_0[rows, cols], staged[:, cols])
+                if i < fine:
+                    nc.sync.dma_start(out_0[rows, :], staged[:])
+
+        def quantise_wv(engine, a):
+            woven = woven_tile()
+            weave(engine, woven[:], wv_raw[a][:])
+            quantise(wv_codes[a][:], wv_scales[a][:], woven[:])
+
+        wv_codes = [tile("wv_codes_%d" % a, [P, N], U32) for a in range(2)]
+        wv_scales = [tile("wv_scales_%d" % a, [P, N], U8) for a in range(2)]
+
+        def values(engines):
+            for i in range(4):
+                staged = tile("values_%d" % i, [P, J], F32)
+                for g in range(2):
+                    acc = table_product(wv_codes, wv_scales, P * i, g, g)
+                    copy(engines[2 * i + g], staged[:, BANK * g : BANK * (g + 1)], acc[:])
+                nc.sync.dma_start(out_1[P * i : P * (i + 1), :], staged[:])
+
+        weave_x("S", 0, 0, 0, 0, 128)
+        weave_x("V", 0, 0, 0, 128, 256)
+        order_r8_scales(0)
+        quantise_x(0, 0, 0, 256)
+        order_r8(0, 0)
+        order_r8_scales(1)
+        order_r8(0, 1)
+        weave_x("S", 0, 0, 256, 256, 384)
+        weave_x("V", 0, 0, 256, 384, 512)
+        quantise_x(0, 0, 256, 512)
+        order_w4_scales(0)
+        order_w4(0)
+        accs = open_first_half()
+        weave_x("S", 0, 1, 0, 0, 256)
+        weave_x("V", 0, 1, 0, 256, 512)
+        quantise_x(0, 1, 0, 512)
+        order_w4_scales(1)
+        order_w4(1)
+        order_r8(1, 0)
+        order_r8(1, 1)
+        close_queries(0, accs)
+        weave_x("V", 1, 0, 0, 0, 512)
+        quantise_x(1, 0, 0, 512)
+        gather_scales(0)
+        gather_scales(1)
+        shift_scales(0)
+        shift_scales(1)
+        load_wv()
+        accs = open_second_half(0)
+        quantise_qa(0, 0)
+        weave_x("V", 1, 1, 0, 256, 512)
+        weave_x("S", 1, 1, 0, 0, 256)
+        quantise_x(1, 1, 0, 512)
+        close_queries(1, accs)
+        quantise_qa(0, 1)
+        gather_words(0)
+        part_words(0)
+        early_scores(0, "SSSS")
+        accs = open_second_half(1)
+        close_queries(1, accs)
+        gather_words(1)
+        part_words(1)
+        early_scores(1, "SSSS")
+        quantise_wv("V", 0)
+        quantise_wv("V", 1)
+        quantise_qa(1, 0)
+        quantise_qa(1, 1)
+        values("SSSSSSSS")
+        late_scores("VSVSVSVS", 2)

@@ -19,6 +19,7 @@ ALU = mybir.AluOpType
 P = 128
 PACK = 4
 BANK = 512
+QUARTER = 256
 SCORE_SCALE = 0.03125
 
 
@@ -28,7 +29,7 @@ def tile_list_mlat_resid_relu_kernel(
     nc = tc.nc
     with ExitStack() as ctx:
         keep = ctx.enter_context(tc.tile_pool(name="keep", bufs=1))
-        weaving = ctx.enter_context(tc.tile_pool(name="weaving", bufs=3))
+        weaving = ctx.enter_context(tc.tile_pool(name="weaving", bufs=4))
         psum = ctx.enter_context(tc.psum_pool(name="psum", bufs=4))
 
         def tile(name, shape, dtype):
@@ -64,19 +65,18 @@ def tile_list_mlat_resid_relu_kernel(
         w4s_raw = tile("w4s_raw", [P, 2 * R // 4], I32)
         r8s_raw = tile("r8s_raw", [P, R // 4], I32)
         tabs_raw = tile("tabs_raw", [P, T // 4], I32)
-        tab_s1 = [tile("tab_s1_%d" % g, [P, BANK // 4], I32) for g in range(2)]
-        nc.gpsimd.memset(r8s_raw[:], 0)
+        tab_s1 = tile("tab_s1", [P, J // 4], I32)
+        nc.vector.memset(r8s_raw[:], 0)
         nc.vector.memset(w4s_raw[:], 0)
         nc.gpsimd.memset(tabs_raw[:], 0)
-        for g in range(2):
-            nc.vector.memset(tab_s1[g][:], 0)
+        nc.vector.memset(tab_s1[:], 0)
 
         x_raw = {}
 
-        def load_x(h, a, c0, c1):
-            raw = tile("x_raw_%d_%d_%d" % (h, a, c0), [P, PACK, c1 - c0], F32)
-            nc.sync.dma_start(raw[:], x_rows[a, :, :, BANK * h + c0 : BANK * h + c1])
-            x_raw[(h, a, c0)] = raw
+        def load_x(q, a):
+            raw = tile("x_raw_%d_%d" % (q, a), [P, PACK, QUARTER], F32)
+            nc.sync.dma_start(raw[:], x_rows[a, :, :, QUARTER * q : QUARTER * (q + 1)])
+            x_raw.setdefault((q, a), raw)
 
         w4_raw = [tile("w4_raw_%d" % a, [P, R // 2], I32) for a in range(2)]
         r8_raw = {(a, b): tile("r8_raw_%d_%d" % (a, b), [P, BANK], I32) for a in range(2) for b in range(2)}
@@ -104,25 +104,26 @@ def tile_list_mlat_resid_relu_kernel(
 
         def load_table_scales():
             nc.sync.dma_start(offsets[:], offs)
-            load_stacked_scales(nc.sync, tabs_raw, tab_scales)
 
         def load_table():
             nc.sync.dma_start(tab_raw[:], tab_words[0].rearrange("p t i -> p (t i)").bitcast(I32))
 
-        load_x(0, 0, 0, 256)
-        load_stacked_scales(nc.sync, r8s_raw, r8_scales)
+        load_stacked_scales(nc.gpsimd, tabs_raw, tab_scales)
+        load_x(0, 0)
         load_r8(0, 0)
+        load_stacked_scales(nc.sync, r8s_raw, r8_scales)
         load_r8(0, 1)
-        load_x(0, 0, 256, 512)
-        load_w4_scales()
         load_w4(0)
-        load_x(0, 1, 0, 512)
+        load_w4_scales()
+        load_x(0, 1)
         load_w4(1)
         load_r8(1, 0)
         load_r8(1, 1)
+        load_x(1, 0)
+        load_x(1, 1)
+        load_x(2, 0)
         load_table_scales()
-        load_x(1, 0, 0, 512)
-        load_x(1, 1, 0, 512)
+        load_x(2, 1)
         load_table()
         wv_raw = [tile("wv_raw_%d" % a, [P, PACK, N], F32) for a in range(2)]
 
@@ -130,25 +131,20 @@ def tile_list_mlat_resid_relu_kernel(
             for a in range(2):
                 nc.sync.dma_start(wv_raw[a][:], wv_rows[a])
 
-        x_woven = {}
-
-        def woven_tile():
-            return weaving.tile([P, BANK, PACK], BF16, name="woven", align_bytes=64)
-
-        x_codes = {(h, a): tile("x_codes_%d_%d" % (h, a), [P, BANK], U32) for h in range(2) for a in range(2)}
-        x_scales = {(h, a): tile("x_scales_%d_%d" % (h, a), [P, BANK], U8) for h in range(2) for a in range(2)}
+        x_codes = {(q, a): tile("x_codes_%d_%d" % (q, a), [P, QUARTER], U32) for q in range(4) for a in range(2)}
+        x_scales = {(q, a): tile("x_scales_%d_%d" % (q, a), [P, QUARTER], U8) for q in range(4) for a in range(2)}
         w4 = [tile("w4_%d" % a, [P, 2 * R], U8) for a in range(2)]
         w4s = [tile("w4s_%d" % a, [P, R], U8) for a in range(2)]
         r8 = {(a, b): tile("r8_%d_%d" % (a, b), [P, BANK], I32) for a in range(2) for b in range(2)}
         r8s = [tile("r8s_%d" % b, [P, BANK], U8) for b in range(2)]
 
-        def weave_x(engine, h, a, load0, c0, c1):
-            if (h, a) not in x_woven:
-                x_woven.setdefault((h, a), woven_tile())
-            weave(engine, x_woven[(h, a)][:, c0:c1, :], x_raw[(h, a, load0)][:, :, c0 - load0 : c1 - load0])
-
-        def quantise_x(h, a, c0, c1):
-            quantise(x_codes[(h, a)][:, c0:c1], x_scales[(h, a)][:, c0:c1], x_woven[(h, a)][:, c0:c1, :])
+        def quantise_x(engines, q, a):
+            woven = weaving.tile([P, QUARTER, PACK], BF16, name="x_woven", align_bytes=64)
+            share = QUARTER // len(engines)
+            for n, engine in enumerate(engines):
+                cols = slice(share * n, share * (n + 1))
+                weave(engine, woven[:, cols, :], x_raw[(q, a)][:, :, cols])
+            quantise(x_codes[(q, a)][:], x_scales[(q, a)][:], woven[:])
 
         def order_w4_scales(a):
             unweave(w4s[a][:], w4s_raw[:].bitcast(U8)[:, R * a : R * (a + 1)], PACK, 16)
@@ -162,65 +158,61 @@ def tile_list_mlat_resid_relu_kernel(
         def order_r8(a, b):
             unweave(r8[(a, b)][:], r8_raw[(a, b)][:], PACK, 4)
 
-        def query_pass(acc, tier, h, a, b, t, start, stop, m0=0, m1=BANK):
-            c0 = 256 * t + P * b
-            if tier == "w4":
-                words = w4[a][:, 2 * c0 : 2 * (c0 + P)].bitcast(FP4X4)
-                scales = w4s[a][:, c0 : c0 + P]
-            else:
-                words = r8[(a, b)][:, P * t : P * (t + 1)].bitcast(FP8X4)
-                scales = r8s[b][4 * a :, P * t : P * (t + 1)]
-            nc.tensor.matmul_mx(
-                out=acc[:, m0:m1], lhsT=words, lhsT_scale=scales,
-                rhs=x_codes[(h, a)][:, m0:m1].bitcast(FP8X4), rhs_scale=x_scales[(h, a)][:, m0:m1],
-                start=start, stop=stop,
-            )
-
-        qa_flat = {(h, b): tile("qa_flat_%d_%d" % (h, b), [P, PACK, BANK], BF16) for h in range(2) for b in range(2)}
-        qa_codes = {(h, b): tile("qa_codes_%d_%d" % (h, b), [P, BANK], U32) for h in range(2) for b in range(2)}
-        qa_scales = {(h, b): tile("qa_scales_%d_%d" % (h, b), [P, BANK], U8) for h in range(2) for b in range(2)}
-        slices = [(b, t) for b in range(2) for t in range(PACK)]
-
         def bank(side):
             return psum.tile([P, BANK], F32, name="bank_%d" % side)
 
-        def open_first_half():
-            accs = {(b, t): bank(b) for b, t in slices}
-            for m0 in (0, 256):
-                for b, t in slices:
-                    query_pass(accs[(b, t)], "r8", 0, 0, b, t, m0 == 0, False, m0, m0 + 256)
-            for b, t in slices:
-                query_pass(accs[(b, t)], "w4", 0, 0, b, t, False, False)
-            return accs
-
-        def open_second_half(b):
-            accs = {(b, t): bank(0) for t in range(PACK)}
+        def query_passes(acc, tier, i, a, b, start=False, stop=False):
+            h, m0 = i // 2, P * (i % 2)
             for t in range(PACK):
-                query_pass(accs[(b, t)], "r8", 1, 0, b, t, True, False)
-                query_pass(accs[(b, t)], "w4", 1, 0, b, t, False, False)
+                if tier == "w4":
+                    c0 = 256 * t + P * b
+                    words = w4[a][:, 2 * c0 : 2 * (c0 + P)].bitcast(FP4X4)
+                    scales = w4s[a][:, c0 : c0 + P]
+                else:
+                    words = r8[(a, b)][:, P * t : P * (t + 1)].bitcast(FP8X4)
+                    scales = r8s[b][4 * a :, P * t : P * (t + 1)]
+                nc.tensor.matmul_mx(
+                    out=acc[:, P * t : P * (t + 1)], lhsT=words, lhsT_scale=scales,
+                    rhs=x_codes[(h, a)][:, m0 : m0 + P].bitcast(FP8X4), rhs_scale=x_scales[(h, a)][:, m0 : m0 + P],
+                    start=start and t == 0, stop=stop and t == PACK - 1,
+                )
+
+        qa_woven = [tile("qa_woven_%d" % i, [P, 2 * P, PACK], BF16) for i in range(8)]
+        qa_codes = [tile("qa_codes_%d" % i, [P, 2 * P], U32) for i in range(8)]
+        qa_scales = [tile("qa_scales_%d" % i, [P, 2 * P], U8) for i in range(8)]
+
+        def open_first_pair():
+            accs = {(i, b): bank(0) for i in range(2) for b in range(2)}
+            for tier in ("r8", "w4"):
+                for b in range(2):
+                    for i in range(2):
+                        query_passes(accs[(i, b)], tier, i, 0, b, start=(tier == "r8"))
             return accs
 
-        def close_queries(h, accs):
-            for b, t in accs:
-                query_pass(accs[(b, t)], "w4", h, 1, b, t, False, False)
-                query_pass(accs[(b, t)], "r8", h, 1, b, t, False, True)
-                copy("S", qa_flat[(h, b)][:, t, :], accs[(b, t)][:])
+        def close_queries(acc, i, b):
+            query_passes(acc, "w4", i, 1, b)
+            query_passes(acc, "r8", i, 1, b, stop=True)
+            copy("S", qa_woven[i][:, P * b : P * (b + 1), :], acc[:].rearrange("p (t m) -> p m t", t=PACK))
+            if b == 1:
+                quantise(qa_codes[i][:], qa_scales[i][:], qa_woven[i][:])
 
-        def quantise_qa(h, b):
-            woven = woven_tile()
-            weave("V", woven[:], qa_flat[(h, b)][:])
-            quantise(qa_codes[(h, b)][:], qa_scales[(h, b)][:], woven[:])
+        def queries(i):
+            for b in range(2):
+                acc = bank(0)
+                query_passes(acc, "r8", i, 0, b, start=True)
+                query_passes(acc, "w4", i, 0, b)
+                close_queries(acc, i, b)
 
         picked = [tile("picked_%d" % g, [P, BANK], U32) for g in range(2)]
         tab = [tile("tab_%d" % g, [P, 2 * 2 * BANK], U8) for g in range(2)]
-        tab_s0 = [tile("tab_s0_%d" % g, [P, BANK], U8) for g in range(2)]
+        tab_s0 = tile("tab_s0", [P, J], U8)
 
         def gather_scales(g):
-            nc.vector.tensor_copy(tab_s0[g][:], tabs_raw[:].bitcast(U8).indirect(offsets[:, 32 * g : 32 * (g + 1)]))
+            nc.vector.tensor_copy(tab_s0[:, BANK * g : BANK * (g + 1)], tabs_raw[:].bitcast(U8).indirect(offsets[:, 32 * g : 32 * (g + 1)]))
 
-        def shift_scales(g):
+        def shift_scales():
             for p0, rows in ((0, 64), (64, 32), (96, 4)):
-                nc.sync.dma_start(tab_s1[g][p0 : p0 + rows, :], tab_s0[g][:].bitcast(I32)[p0 + 4 : p0 + 4 + rows, :])
+                nc.sync.dma_start(tab_s1[p0 : p0 + rows, :], tab_s0[:].bitcast(I32)[p0 + 4 : p0 + 4 + rows, :])
 
         def gather_words(g):
             nc.vector.tensor_copy(picked[g][:], tab_raw[:].bitcast(U32).indirect(offsets[:, 32 * g : 32 * (g + 1)]))
@@ -228,107 +220,102 @@ def tile_list_mlat_resid_relu_kernel(
         def part_words(g):
             unweave(tab[g][:].bitcast(U16), picked[g][:].bitcast(U16), 2, 8)
 
-        def table_product(codes, scales, c0, g, side):
-            acc = bank(side)
+        def table_product(operand, g):
+            acc = bank(1)
             for a in range(2):
-                plane = tab_s0[g][:] if a == 0 else tab_s1[g][:].bitcast(U8)
+                codes, scales = operand(a)
+                plane = tab_s0[:] if a == 0 else tab_s1[:].bitcast(U8)
                 nc.tensor.matmul_mx(
-                    out=acc[:], lhsT=codes[a][:, c0 : c0 + P].bitcast(FP8X4), lhsT_scale=scales[a][:, c0 : c0 + P],
+                    out=acc[:], lhsT=codes.bitcast(FP8X4), lhsT_scale=scales,
                     rhs=tab[g][:, 2 * BANK * a : 2 * BANK * (a + 1)].bitcast(FP4X4),
-                    rhs_scale=plane,
+                    rhs_scale=plane[:, BANK * g : BANK * (g + 1)],
                     start=(a == 0), stop=(a == 1),
                 )
             return acc
 
-        def score_tile(engine, h, i, g, side, staged):
-            codes = [qa_codes[(h, b)] for b in range(2)]
-            scales = [qa_scales[(h, b)] for b in range(2)]
-            acc = table_product(codes, scales, P * i, g, side)
-            if engine == "S":
-                nc.scalar.activation(staged, acc[:], ACT.Relu, scale=SCORE_SCALE)
-            else:
-                nc.vector.tensor_scalar(staged, acc[:], 0.0, SCORE_SCALE, ALU.max, ALU.mult)
-
-        def early_scores(g, engines):
-            for i in range(4):
-                staged = tile("scores_0_%d_%d" % (i, g), [P, BANK], F32)
-                score_tile(engines[i], 0, i, g, 1, staged[:])
-                nc.sync.dma_start(out_0[P * i : P * (i + 1), BANK * g : BANK * (g + 1)], staged[:])
-
-        def late_scores(engines, fine):
-            for i in range(4):
-                rows = slice(BANK + P * i, BANK + P * (i + 1))
-                staged = tile("scores_1_%d" % i, [P, J], F32)
-                for g in range(2):
-                    cols = slice(BANK * g, BANK * (g + 1))
-                    score_tile(engines[2 * i + g], 1, i, g, g, staged[:, cols])
-                    if i >= fine:
-                        nc.sync.dma_start(out_0[rows, cols], staged[:, cols])
-                if i < fine:
-                    nc.sync.dma_start(out_0[rows, :], staged[:])
+        def scores(i, engines, split=False):
+            rows = slice(P * i, P * (i + 1))
+            staged = tile("scores_%d" % i, [P, J], F32)
+            for g in range(2):
+                cols = slice(BANK * g, BANK * (g + 1))
+                acc = table_product(lambda a: (qa_codes[i][:, P * a : P * (a + 1)], qa_scales[i][:, P * a : P * (a + 1)]), g)
+                if engines[g] == "S":
+                    nc.scalar.activation(staged[:, cols], acc[:], ACT.Relu, scale=SCORE_SCALE)
+                else:
+                    nc.vector.tensor_scalar(staged[:, cols], acc[:], 0.0, SCORE_SCALE, ALU.max, ALU.mult)
+                if split:
+                    nc.sync.dma_start(out_0[rows, cols], staged[:, cols])
+            if not split:
+                nc.sync.dma_start(out_0[rows, :], staged[:])
 
         def quantise_wv(engine, a):
-            woven = woven_tile()
+            woven = tile("wv_woven_%d" % a, [P, N, PACK], BF16)
             weave(engine, woven[:], wv_raw[a][:])
             quantise(wv_codes[a][:], wv_scales[a][:], woven[:])
 
         wv_codes = [tile("wv_codes_%d" % a, [P, N], U32) for a in range(2)]
         wv_scales = [tile("wv_scales_%d" % a, [P, N], U8) for a in range(2)]
 
-        def values(engines):
-            for i in range(4):
-                staged = tile("values_%d" % i, [P, J], F32)
-                for g in range(2):
-                    acc = table_product(wv_codes, wv_scales, P * i, g, g)
-                    copy(engines[2 * i + g], staged[:, BANK * g : BANK * (g + 1)], acc[:])
-                nc.sync.dma_start(out_1[P * i : P * (i + 1), :], staged[:])
+        def values(i, engines, split=False):
+            rows = slice(P * i, P * (i + 1))
+            staged = tile("values_%d" % i, [P, J], F32)
+            for g in range(2):
+                acc = table_product(lambda a: (wv_codes[a][:, rows], wv_scales[a][:, rows]), g)
+                cols = slice(BANK * g, BANK * (g + 1))
+                copy(engines[g], staged[:, cols], acc[:])
+                if split:
+                    nc.sync.dma_start(out_1[rows, cols], staged[:, cols])
+            if not split:
+                nc.sync.dma_start(out_1[rows, :], staged[:])
 
-        weave_x("S", 0, 0, 0, 0, 128)
-        weave_x("V", 0, 0, 0, 128, 256)
-        order_r8_scales(0)
-        quantise_x(0, 0, 0, 256)
         order_r8(0, 0)
+        quantise_x("SV", 0, 0)
+        order_r8_scales(0)
         order_r8_scales(1)
         order_r8(0, 1)
-        weave_x("S", 0, 0, 256, 256, 384)
-        weave_x("V", 0, 0, 256, 384, 512)
-        quantise_x(0, 0, 256, 512)
-        order_w4_scales(0)
         order_w4(0)
-        accs = open_first_half()
-        weave_x("S", 0, 1, 0, 0, 256)
-        weave_x("V", 0, 1, 0, 256, 512)
-        quantise_x(0, 1, 0, 512)
+        order_w4_scales(0)
+        accs = open_first_pair()
+        quantise_x("SV", 0, 1)
         order_w4_scales(1)
         order_w4(1)
         order_r8(1, 0)
         order_r8(1, 1)
-        close_queries(0, accs)
-        weave_x("V", 1, 0, 0, 0, 512)
-        quantise_x(1, 0, 0, 512)
+        for i, b in accs:
+            close_queries(accs[(i, b)], i, b)
+        quantise_x("V", 1, 0)
+        quantise_x("V", 1, 1)
+        queries(2)
+        queries(3)
         gather_scales(0)
         gather_scales(1)
-        shift_scales(0)
-        shift_scales(1)
+        shift_scales()
+        load_x(3, 0)
+        load_x(3, 1)
         load_wv()
-        accs = open_second_half(0)
-        quantise_qa(0, 0)
-        weave_x("V", 1, 1, 0, 256, 512)
-        weave_x("S", 1, 1, 0, 0, 256)
-        quantise_x(1, 1, 0, 512)
-        close_queries(1, accs)
-        quantise_qa(0, 1)
+        quantise_x("S", 2, 0)
+        quantise_x("S", 2, 1)
+        queries(4)
+        queries(5)
         gather_words(0)
         part_words(0)
-        early_scores(0, "SSSS")
-        accs = open_second_half(1)
-        close_queries(1, accs)
         gather_words(1)
         part_words(1)
-        early_scores(1, "SSSS")
+        quantise_x("S", 3, 0)
+        quantise_x("S", 3, 1)
+        scores(0, "SV")
+        scores(1, "SV")
+        scores(2, "SV")
+        scores(3, "SV")
+        queries(6)
         quantise_wv("V", 0)
         quantise_wv("V", 1)
-        quantise_qa(1, 0)
-        quantise_qa(1, 1)
-        values("SSSSSSSS")
-        late_scores("VSVSVSVS", 2)
+        scores(4, "SV")
+        scores(5, "SV")
+        values(0, "SV")
+        values(1, "SV")
+        scores(6, "SV")
+        queries(7)
+        values(2, "SV", split=True)
+        values(3, "SV", split=True)
+        scores(7, "SV", split=True)

@@ -18,9 +18,14 @@ ALU = mybir.AluOpType
 
 P = 128
 PACK = 4
+PASS = P * PACK
 BANK = 512
-QUARTER = 256
+QUARTER = M // 4
+LINE = 16
 SCORE_SCALE = 0.03125
+SCALE_ROWS = 4
+QUADRANT = 32
+SCALAR, VECTOR = "S", "V"
 
 
 def tile_list_mlat_resid_relu_kernel(
@@ -29,293 +34,273 @@ def tile_list_mlat_resid_relu_kernel(
     nc = tc.nc
     with ExitStack() as ctx:
         keep = ctx.enter_context(tc.tile_pool(name="keep", bufs=1))
-        weaving = ctx.enter_context(tc.tile_pool(name="weaving", bufs=4))
         psum = ctx.enter_context(tc.psum_pool(name="psum", bufs=4))
 
         def tile(name, shape, dtype):
             return keep.tile(shape, dtype, name=name, align_bytes=64)
 
+        def bank(side):
+            return psum.tile([P, BANK], F32, name="bank_%d" % side)
+
         def copy(engine, out, in_):
-            if engine == "S":
+            if engine == SCALAR:
                 nc.scalar.activation(out, in_, ACT.Copy)
             else:
                 nc.vector.tensor_copy(out, in_)
 
-        def weave(engine, dst, src):
-            copy(
-                engine,
-                dst.rearrange("p (c i) t -> p c t i", i=4),
-                src.rearrange("p t (c i) -> p c t i", i=4),
+        def quantise(name, woven):
+            width = woven.shape[1]
+            codes = tile(name + "_codes", [P, width], U32)
+            scales = tile(name + "_scales", [P, width], U8)
+            nc.vector.quantize_mx(
+                out=codes[:].bitcast(FP8X4), scales=scales[:], in_=woven.rearrange("p c t -> p (c t)")
             )
+            return codes, scales
 
-        def unweave(dst, src, ways, run):
+        def weave_and_quantise(name, raw, engines):
+            width = raw.shape[2]
+            woven = tile(name + "_woven", [P, width, PACK], BF16)
+            share = width // len(engines)
+            for n, engine in enumerate(engines):
+                cols = slice(share * n, share * (n + 1))
+                copy(
+                    engine,
+                    woven[:, cols, :].rearrange("p (c i) t -> p c t i", i=4),
+                    raw[:, :, cols].rearrange("p t (c i) -> p c t i", i=4),
+                )
+            return quantise(name, woven[:])
+
+        def deal(dst, src, ways, run):
             nc.vector.tensor_copy(
                 dst.rearrange("p (t c i) -> p c t i", t=ways, i=run),
                 src.rearrange("p (c i t) -> p c t i", t=ways, i=run),
             )
 
-        def quantise(codes, scales, woven):
-            nc.vector.quantize_mx(
-                out=codes.bitcast(FP8X4), scales=scales, in_=woven.rearrange("p m t -> p (m t)")
-            )
+        w4s_raw = tile("w4s_raw", [P, 2 * R // 4], I32)
+        r8s_raw = tile("r8s_raw", [P, R // 4], I32)
+        tabs_raw = tile("tabs_raw", [P, T // 4], I32)
+        picked_s1 = tile("picked_s1", [P, J // 4], I32)
+        nc.vector.memset(r8s_raw[:], 0)
+        nc.vector.memset(w4s_raw[:], 0)
+        nc.gpsimd.memset(tabs_raw[:], 0)
+        nc.vector.memset(picked_s1[:], 0)
+
+        def load(name, src):
+            raw = tile(name, list(src.shape), src.dtype)
+            nc.sync.dma_start(raw[:], src)
+            return raw
 
         x_rows = x.rearrange("(a p t) m -> a p t m", a=2, t=PACK)
         wv_rows = wv.rearrange("(a p t) n -> a p t n", a=2, t=PACK)
 
-        w4s_raw = tile("w4s_raw", [P, 2 * R // 4], I32)
-        r8s_raw = tile("r8s_raw", [P, R // 4], I32)
-        tabs_raw = tile("tabs_raw", [P, T // 4], I32)
-        tab_s1 = tile("tab_s1", [P, J // 4], I32)
-        nc.vector.memset(r8s_raw[:], 0)
-        nc.vector.memset(w4s_raw[:], 0)
-        nc.gpsimd.memset(tabs_raw[:], 0)
-        nc.vector.memset(tab_s1[:], 0)
-
-        x_raw = {}
-
         def load_x(q, a):
-            raw = tile("x_raw_%d_%d" % (q, a), [P, PACK, QUARTER], F32)
-            nc.sync.dma_start(raw[:], x_rows[a, :, :, QUARTER * q : QUARTER * (q + 1)])
-            x_raw.setdefault((q, a), raw)
-
-        w4_raw = [tile("w4_raw_%d" % a, [P, R // 2], I32) for a in range(2)]
-        r8_raw = {(a, b): tile("r8_raw_%d_%d" % (a, b), [P, BANK], I32) for a in range(2) for b in range(2)}
+            return load("x_raw_%d_%d" % (q, a), x_rows[a, :, :, QUARTER * q : QUARTER * (q + 1)])
 
         def load_w4(a):
-            nc.sync.dma_start(w4_raw[a][:], w4_words[a].bitcast(I32))
+            return load("w4_raw_%d" % a, w4_words[a].bitcast(I32))
 
         def load_r8(a, b):
             words = r8_words[a].rearrange("p r i -> p (r i)").bitcast(I32)
-            nc.sync.dma_start(r8_raw[(a, b)][:], words[:, BANK * b : BANK * (b + 1)])
+            return load("r8_raw_%d_%d" % (a, b), words[:, PASS * b : PASS * (b + 1)])
+
+        def quadrant_rows(scales, quad):
+            return scales.bitcast(I32)[:, SCALE_ROWS * quad : SCALE_ROWS * (quad + 1), :]
 
         def load_stacked_scales(queue, raw, scales):
-            for q in range(4):
-                queue.dma_start(raw[32 * q : 32 * q + 8, :], scales.bitcast(I32)[:, 4 * q : 4 * q + 4, :])
+            for quad in range(P // QUADRANT):
+                queue.dma_start(raw[QUADRANT * quad : QUADRANT * quad + 2 * SCALE_ROWS, :], quadrant_rows(scales, quad))
 
-        def load_w4_scales():
-            for q in range(4):
-                nc.sync.dma_start(
-                    w4s_raw[32 * q : 32 * q + 4, :].rearrange("p (a r) -> p a r", a=2),
-                    w4_scales.bitcast(I32)[:, 4 * q : 4 * q + 4, :].rearrange("a q r -> q a r"),
-                )
-
-        offsets = keep.tile([P, J // 16], U16, name="offsets")
-        tab_raw = tile("tab_raw", [P, T], I32)
-
-        def load_table_scales():
-            nc.sync.dma_start(offsets[:], offs)
-
-        def load_table():
-            nc.sync.dma_start(tab_raw[:], tab_words[0].rearrange("p t i -> p (t i)").bitcast(I32))
-
+        x_raw, r8_raw, w4_raw = {}, {}, {}
         load_stacked_scales(nc.gpsimd, tabs_raw, tab_scales)
-        load_x(0, 0)
-        load_r8(0, 0)
+        x_raw[0, 0] = load_x(0, 0)
+        r8_raw[0, 0] = load_r8(0, 0)
         load_stacked_scales(nc.sync, r8s_raw, r8_scales)
-        load_r8(0, 1)
-        load_w4(0)
-        load_w4_scales()
-        load_x(0, 1)
-        load_w4(1)
-        load_r8(1, 0)
-        load_r8(1, 1)
-        load_x(1, 0)
-        load_x(1, 1)
-        load_x(2, 0)
-        load_table_scales()
-        load_x(2, 1)
-        load_table()
-        wv_raw = [tile("wv_raw_%d" % a, [P, PACK, N], F32) for a in range(2)]
+        r8_raw[0, 1] = load_r8(0, 1)
+        w4_raw[0] = load_w4(0)
+        for quad in range(P // QUADRANT):
+            nc.sync.dma_start(
+                w4s_raw[QUADRANT * quad : QUADRANT * quad + SCALE_ROWS, :].rearrange("p (a r) -> p a r", a=2),
+                quadrant_rows(w4_scales, quad).rearrange("a row r -> row a r"),
+            )
+        x_raw[0, 1] = load_x(0, 1)
+        r8_raw[1, 0] = load_r8(1, 0)
+        r8_raw[1, 1] = load_r8(1, 1)
+        w4_raw[1] = load_w4(1)
+        x_raw[1, 0] = load_x(1, 0)
+        x_raw[1, 1] = load_x(1, 1)
+        x_raw[2, 0] = load_x(2, 0)
+        offsets = keep.tile([P, J // 16], U16, name="offsets")
+        nc.sync.dma_start(offsets[:], offs)
+        x_raw[2, 1] = load_x(2, 1)
+        tab_raw = load("tab_raw", tab_words[0].rearrange("p t i -> p (t i)").bitcast(I32))
 
-        def load_wv():
-            for a in range(2):
-                nc.sync.dma_start(wv_raw[a][:], wv_rows[a])
-
-        x_codes = {(q, a): tile("x_codes_%d_%d" % (q, a), [P, QUARTER], U32) for q in range(4) for a in range(2)}
-        x_scales = {(q, a): tile("x_scales_%d_%d" % (q, a), [P, QUARTER], U8) for q in range(4) for a in range(2)}
+        xq, qa = {}, {}
         w4 = [tile("w4_%d" % a, [P, 2 * R], U8) for a in range(2)]
         w4s = [tile("w4s_%d" % a, [P, R], U8) for a in range(2)]
-        r8 = {(a, b): tile("r8_%d_%d" % (a, b), [P, BANK], I32) for a in range(2) for b in range(2)}
-        r8s = [tile("r8s_%d" % b, [P, BANK], U8) for b in range(2)]
+        r8 = {(a, b): tile("r8_%d_%d" % (a, b), [P, PASS], I32) for a in range(2) for b in range(2)}
+        r8s = [tile("r8s_%d" % b, [P, PASS], U8) for b in range(2)]
 
-        def quantise_x(engines, q, a):
-            woven = weaving.tile([P, QUARTER, PACK], BF16, name="x_woven", align_bytes=64)
-            share = QUARTER // len(engines)
-            for n, engine in enumerate(engines):
-                cols = slice(share * n, share * (n + 1))
-                weave(engine, woven[:, cols, :], x_raw[(q, a)][:, :, cols])
-            quantise(x_codes[(q, a)][:], x_scales[(q, a)][:], woven[:])
-
-        def order_w4_scales(a):
-            unweave(w4s[a][:], w4s_raw[:].bitcast(U8)[:, R * a : R * (a + 1)], PACK, 16)
+        def quantise_x(q, a, engines):
+            xq[q, a] = weave_and_quantise("x_%d_%d" % (q, a), x_raw[q, a], engines)
 
         def order_w4(a):
-            unweave(w4[a][:].bitcast(U16), w4_raw[a][:].bitcast(U16), PACK, 8)
+            deal(w4[a][:].bitcast(U16), w4_raw[a][:].bitcast(U16), PACK, LINE // 2)
 
-        def order_r8_scales(b):
-            unweave(r8s[b][:], r8s_raw[:].bitcast(U8)[:, BANK * b : BANK * (b + 1)], PACK, 16)
+        def order_w4_scales(a):
+            deal(w4s[a][:], w4s_raw[:].bitcast(U8)[:, R * a : R * (a + 1)], PACK, LINE)
 
         def order_r8(a, b):
-            unweave(r8[(a, b)][:], r8_raw[(a, b)][:], PACK, 4)
+            deal(r8[a, b][:], r8_raw[a, b][:], PACK, LINE // 4)
 
-        def bank(side):
-            return psum.tile([P, BANK], F32, name="bank_%d" % side)
+        def order_r8_scales(b):
+            deal(r8s[b][:], r8s_raw[:].bitcast(U8)[:, PASS * b : PASS * (b + 1)], PACK, LINE)
 
-        def query_passes(acc, tier, i, a, b, start=False, stop=False):
-            h, m0 = i // 2, P * (i % 2)
+        def query_pass(out, tier, q, a, b, t, cols, start, stop):
+            if tier == "w4":
+                c0 = 2 * P * t + P * b
+                words, scales = w4[a][:, 2 * c0 : 2 * (c0 + P)].bitcast(FP4X4), w4s[a][:, c0 : c0 + P]
+            else:
+                words = r8[a, b][:, P * t : P * (t + 1)].bitcast(FP8X4)
+                scales = r8s[b][SCALE_ROWS * a :, P * t : P * (t + 1)]
+            codes, code_scales = xq[q, a]
+            nc.tensor.matmul_mx(
+                out=out,
+                lhsT=words,
+                lhsT_scale=scales,
+                rhs=codes[:, cols].bitcast(FP8X4),
+                rhs_scale=code_scales[:, cols],
+                start=start,
+                stop=stop,
+            )
+
+        def tier_passes(acc, tier, i, a, b, start=False, stop=False):
+            cols = slice(P * (i % 2), P * (i % 2 + 1))
             for t in range(PACK):
-                if tier == "w4":
-                    c0 = 256 * t + P * b
-                    words = w4[a][:, 2 * c0 : 2 * (c0 + P)].bitcast(FP4X4)
-                    scales = w4s[a][:, c0 : c0 + P]
-                else:
-                    words = r8[(a, b)][:, P * t : P * (t + 1)].bitcast(FP8X4)
-                    scales = r8s[b][4 * a :, P * t : P * (t + 1)]
-                nc.tensor.matmul_mx(
-                    out=acc[:, P * t : P * (t + 1)], lhsT=words, lhsT_scale=scales,
-                    rhs=x_codes[(h, a)][:, m0 : m0 + P].bitcast(FP8X4), rhs_scale=x_scales[(h, a)][:, m0 : m0 + P],
-                    start=start and t == 0, stop=stop and t == PACK - 1,
-                )
+                out = acc[:, P * t : P * (t + 1)]
+                query_pass(out, tier, i // 2, a, b, t, cols, start and t == 0, stop and t == PACK - 1)
 
-        qa_woven = [tile("qa_woven_%d" % i, [P, 2 * P, PACK], BF16) for i in range(8)]
-        qa_codes = [tile("qa_codes_%d" % i, [P, 2 * P], U32) for i in range(8)]
-        qa_scales = [tile("qa_scales_%d" % i, [P, 2 * P], U8) for i in range(8)]
+        qa_woven = [tile("qa_%d_woven" % i, [P, 2 * P, PACK], BF16) for i in range(M // P)]
 
-        def open_first_pair():
-            accs = {(i, b): bank(0) for i in range(2) for b in range(2)}
-            for tier in ("r8", "w4"):
-                for b in range(2):
-                    for i in range(2):
-                        query_passes(accs[(i, b)], tier, i, 0, b, start=(tier == "r8"))
-            return accs
+        def empty_bank(acc, i, b):
+            copy(SCALAR, qa_woven[i][:, P * b : P * (b + 1), :], acc[:].rearrange("p (t m) -> p m t", t=PACK))
 
-        def close_queries(acc, i, b):
-            query_passes(acc, "w4", i, 1, b)
-            query_passes(acc, "r8", i, 1, b, stop=True)
-            copy("S", qa_woven[i][:, P * b : P * (b + 1), :], acc[:].rearrange("p (t m) -> p m t", t=PACK))
-            if b == 1:
-                quantise(qa_codes[i][:], qa_scales[i][:], qa_woven[i][:])
+        def quantise_qa(i):
+            codes, scales = quantise("qa_%d" % i, qa_woven[i][:])
+            qa[i] = [(codes[:, P * b : P * (b + 1)], scales[:, P * b : P * (b + 1)]) for b in range(2)]
 
-        def queries(i):
+        def queries(i, side):
             for b in range(2):
-                acc = bank(0)
-                query_passes(acc, "r8", i, 0, b, start=True)
-                query_passes(acc, "w4", i, 0, b)
-                close_queries(acc, i, b)
+                acc = bank(side)
+                tier_passes(acc, "r8", i, 0, b, start=True)
+                tier_passes(acc, "w4", i, 0, b)
+                tier_passes(acc, "r8", i, 1, b)
+                tier_passes(acc, "w4", i, 1, b, stop=True)
+                empty_bank(acc, i, b)
+            quantise_qa(i)
 
-        picked = [tile("picked_%d" % g, [P, BANK], U32) for g in range(2)]
-        tab = [tile("tab_%d" % g, [P, 2 * 2 * BANK], U8) for g in range(2)]
-        tab_s0 = tile("tab_s0", [P, J], U8)
+        picked_s0 = tile("picked_s0", [P, J], U8)
+        table = [tile("table_%d" % g, [P, 2 * 2 * BANK], U8) for g in range(2)]
 
-        def gather_scales(g):
-            nc.vector.tensor_copy(tab_s0[:, BANK * g : BANK * (g + 1)], tabs_raw[:].bitcast(U8).indirect(offsets[:, 32 * g : 32 * (g + 1)]))
-
-        def shift_scales():
-            for p0, rows in ((0, 64), (64, 32), (96, 4)):
-                nc.sync.dma_start(tab_s1[p0 : p0 + rows, :], tab_s0[:].bitcast(I32)[p0 + 4 : p0 + 4 + rows, :])
+        def listed(window, g):
+            return window.indirect(offsets[:, BANK // 16 * g : BANK // 16 * (g + 1)])
 
         def gather_words(g):
-            nc.vector.tensor_copy(picked[g][:], tab_raw[:].bitcast(U32).indirect(offsets[:, 32 * g : 32 * (g + 1)]))
+            picked = tile("picked_%d" % g, [P, BANK], U32)
+            nc.vector.tensor_copy(picked[:], listed(tab_raw[:].bitcast(U32), g))
+            deal(table[g][:].bitcast(U16), picked[:].bitcast(U16), 2, LINE // 2)
 
-        def part_words(g):
-            unweave(tab[g][:].bitcast(U16), picked[g][:].bitcast(U16), 2, 8)
+        def relu_scaled(engine, out, in_):
+            if engine == SCALAR:
+                nc.scalar.activation(out, in_, ACT.Relu, scale=SCORE_SCALE)
+            else:
+                nc.vector.tensor_scalar(out, in_, 0.0, SCORE_SCALE, ALU.max, ALU.mult)
 
-        def table_product(operand, g):
-            acc = bank(1)
-            for a in range(2):
-                codes, scales = operand(a)
-                plane = tab_s0[:] if a == 0 else tab_s1[:].bitcast(U8)
-                nc.tensor.matmul_mx(
-                    out=acc[:], lhsT=codes.bitcast(FP8X4), lhsT_scale=scales,
-                    rhs=tab[g][:, 2 * BANK * a : 2 * BANK * (a + 1)].bitcast(FP4X4),
-                    rhs_scale=plane[:, BANK * g : BANK * (g + 1)],
-                    start=(a == 0), stop=(a == 1),
-                )
-            return acc
-
-        def scores(i, engines, split=False):
-            rows = slice(P * i, P * (i + 1))
-            staged = tile("scores_%d" % i, [P, J], F32)
-            for g in range(2):
+        def table_rows(name, stationary, leave, rows, split):
+            staged = tile(name, [P, J], F32)
+            for g, engine in enumerate((SCALAR, VECTOR)):
                 cols = slice(BANK * g, BANK * (g + 1))
-                acc = table_product(lambda a: (qa_codes[i][:, P * a : P * (a + 1)], qa_scales[i][:, P * a : P * (a + 1)]), g)
-                if engines[g] == "S":
-                    nc.scalar.activation(staged[:, cols], acc[:], ACT.Relu, scale=SCORE_SCALE)
-                else:
-                    nc.vector.tensor_scalar(staged[:, cols], acc[:], 0.0, SCORE_SCALE, ALU.max, ALU.mult)
+                acc = bank(1)
+                for a, scale_bytes in enumerate((picked_s0[:], picked_s1[:].bitcast(U8))):
+                    nc.tensor.matmul_mx(
+                        out=acc[:],
+                        lhsT=stationary[a][0].bitcast(FP8X4),
+                        lhsT_scale=stationary[a][1],
+                        rhs=table[g][:, 2 * BANK * a : 2 * BANK * (a + 1)].bitcast(FP4X4),
+                        rhs_scale=scale_bytes[:, cols],
+                        start=(a == 0),
+                        stop=(a == 1),
+                    )
+                leave(engine, staged[:, cols], acc[:])
                 if split:
-                    nc.sync.dma_start(out_0[rows, cols], staged[:, cols])
+                    nc.sync.dma_start(rows[:, cols], staged[:, cols])
             if not split:
-                nc.sync.dma_start(out_0[rows, :], staged[:])
+                nc.sync.dma_start(rows, staged[:])
 
-        def quantise_wv(engine, a):
-            woven = tile("wv_woven_%d" % a, [P, N, PACK], BF16)
-            weave(engine, woven[:], wv_raw[a][:])
-            quantise(wv_codes[a][:], wv_scales[a][:], woven[:])
+        def scores(i, split=False):
+            table_rows("scores_%d" % i, qa[i], relu_scaled, out_0[P * i : P * (i + 1), :], split)
 
-        wv_codes = [tile("wv_codes_%d" % a, [P, N], U32) for a in range(2)]
-        wv_scales = [tile("wv_scales_%d" % a, [P, N], U8) for a in range(2)]
-
-        def values(i, engines, split=False):
-            rows = slice(P * i, P * (i + 1))
-            staged = tile("values_%d" % i, [P, J], F32)
-            for g in range(2):
-                acc = table_product(lambda a: (wv_codes[a][:, rows], wv_scales[a][:, rows]), g)
-                cols = slice(BANK * g, BANK * (g + 1))
-                copy(engines[g], staged[:, cols], acc[:])
-                if split:
-                    nc.sync.dma_start(out_1[rows, cols], staged[:, cols])
-            if not split:
-                nc.sync.dma_start(out_1[rows, :], staged[:])
+        def values(i, split=False):
+            cols = slice(P * i, P * (i + 1))
+            stationary = [(codes[:, cols], scales[:, cols]) for codes, scales in wvq]
+            table_rows("values_%d" % i, stationary, copy, out_1[cols, :], split)
 
         order_r8(0, 0)
-        quantise_x("SV", 0, 0)
+        quantise_x(0, 0, (SCALAR, VECTOR))
         order_r8_scales(0)
         order_r8_scales(1)
         order_r8(0, 1)
         order_w4(0)
         order_w4_scales(0)
-        accs = open_first_pair()
-        quantise_x("SV", 0, 1)
+        first = {(i, b): bank(0) for b in range(2) for i in range(2)}
+        for tier in ("r8", "w4"):
+            for i, b in first:
+                tier_passes(first[i, b], tier, i, 0, b, start=(tier == "r8"))
+        quantise_x(0, 1, (SCALAR, VECTOR))
         order_w4_scales(1)
-        order_w4(1)
         order_r8(1, 0)
         order_r8(1, 1)
-        for i, b in accs:
-            close_queries(accs[(i, b)], i, b)
-        quantise_x("V", 1, 0)
-        quantise_x("V", 1, 1)
-        queries(2)
-        queries(3)
-        gather_scales(0)
-        gather_scales(1)
-        shift_scales()
-        load_x(3, 0)
-        load_x(3, 1)
-        load_wv()
-        quantise_x("S", 2, 0)
-        quantise_x("S", 2, 1)
-        queries(4)
-        queries(5)
+        order_w4(1)
+        for i, b in first:
+            tier_passes(first[i, b], "r8", i, 1, b)
+        for i, b in first:
+            tier_passes(first[i, b], "w4", i, 1, b, stop=True)
+            empty_bank(first[i, b], i, b)
+
+        quantise_x(1, 0, (VECTOR,))
+        quantise_x(1, 1, (VECTOR,))
+        quantise_qa(0)
+        quantise_qa(1)
+        queries(2, 1)
+        queries(3, 1)
+
+        for g in range(2):
+            nc.vector.tensor_copy(picked_s0[:, BANK * g : BANK * (g + 1)], listed(tabs_raw[:].bitcast(U8), g))
+        for p0, rows in ((0, 64), (64, 32), (96, 4)):
+            stacked = picked_s0[:].bitcast(I32)[p0 + SCALE_ROWS : p0 + SCALE_ROWS + rows, :]
+            nc.sync.dma_start(picked_s1[p0 : p0 + rows, :], stacked)
+        x_raw[3, 0] = load_x(3, 0)
+        x_raw[3, 1] = load_x(3, 1)
+        wv_raw = [load("wv_raw_%d" % a, wv_rows[a]) for a in range(2)]
+
+        quantise_x(2, 0, (SCALAR,))
+        quantise_x(2, 1, (SCALAR,))
+        queries(4, 0)
+        queries(5, 0)
         gather_words(0)
-        part_words(0)
         gather_words(1)
-        part_words(1)
-        quantise_x("S", 3, 0)
-        quantise_x("S", 3, 1)
-        scores(0, "SV")
-        scores(1, "SV")
-        scores(2, "SV")
-        scores(3, "SV")
-        queries(6)
-        quantise_wv("V", 0)
-        quantise_wv("V", 1)
-        scores(4, "SV")
-        scores(5, "SV")
-        values(0, "SV")
-        values(1, "SV")
-        scores(6, "SV")
-        queries(7)
-        values(2, "SV", split=True)
-        values(3, "SV", split=True)
-        scores(7, "SV", split=True)
+        quantise_x(3, 0, (SCALAR,))
+        quantise_x(3, 1, (SCALAR,))
+
+        for i in range(4):
+            scores(i)
+        queries(6, 0)
+        wvq = [weave_and_quantise("wv_%d" % a, wv_raw[a], (VECTOR,)) for a in range(2)]
+        scores(4)
+        scores(5)
+        values(0)
+        values(1)
+        scores(6)
+        queries(7, 0)
+        values(2, split=True)
+        values(3, split=True)
+        scores(7, split=True)

from contextlib import ExitStack

import concourse.mybir as mybir

K, R, M, T, N, J = 1024, 1024, 1024, 2048, 512, 1024
FLOPS = 2 * (2 * K * R * M + R * M * J + R * N * J)

F32 = mybir.dt.float32
BF16 = mybir.dt.bfloat16
I32 = mybir.dt.int32
U32 = mybir.dt.uint32
U16 = mybir.dt.uint16
U8 = mybir.dt.uint8
FP8X4 = mybir.dt.float8_e4m3fn_x4
FP4X4 = mybir.dt.float4_e2m1fn_x4
ACT = mybir.ActivationFunctionType
ALU = mybir.AluOpType

P = 128
PACK = 4
PASS = P * PACK
BANK = 512
QUARTER = M // 4
LINE = 16
SCORE_SCALE = 0.03125
SCALE_ROWS = 4
QUADRANT = 32
SCALAR, VECTOR = "S", "V"


def tile_list_mlat_resid_relu_kernel(
    tc, x, w4_words, w4_scales, r8_words, r8_scales, tab_words, tab_scales, wv, offs, out_0, out_1
):
    nc = tc.nc
    with ExitStack() as ctx:
        keep = ctx.enter_context(tc.tile_pool(name="keep", bufs=1))
        psum = ctx.enter_context(tc.psum_pool(name="psum", bufs=4))

        def tile(name, shape, dtype):
            return keep.tile(shape, dtype, name=name, align_bytes=64)

        def bank(side):
            return psum.tile([P, BANK], F32, name="bank_%d" % side)

        def copy(engine, out, in_):
            if engine == SCALAR:
                nc.scalar.activation(out, in_, ACT.Copy)
            else:
                nc.vector.tensor_copy(out, in_)

        def quantise(name, woven):
            width = woven.shape[1]
            codes = tile(name + "_codes", [P, width], U32)
            scales = tile(name + "_scales", [P, width], U8)
            nc.vector.quantize_mx(
                out=codes[:].bitcast(FP8X4), scales=scales[:], in_=woven.rearrange("p c t -> p (c t)")
            )
            return codes, scales

        def weave_and_quantise(name, raw, engines):
            width = raw.shape[2]
            woven = tile(name + "_woven", [P, width, PACK], BF16)
            share = width // len(engines)
            for n, engine in enumerate(engines):
                cols = slice(share * n, share * (n + 1))
                copy(
                    engine,
                    woven[:, cols, :].rearrange("p (c i) t -> p c t i", i=4),
                    raw[:, :, cols].rearrange("p t (c i) -> p c t i", i=4),
                )
            return quantise(name, woven[:])

        def deal(dst, src, ways, run):
            nc.vector.tensor_copy(
                dst.rearrange("p (t c i) -> p c t i", t=ways, i=run),
                src.rearrange("p (c i t) -> p c t i", t=ways, i=run),
            )

        w4s_raw = tile("w4s_raw", [P, 2 * R // 4], I32)
        r8s_raw = tile("r8s_raw", [P, R // 4], I32)
        tabs_raw = tile("tabs_raw", [P, T // 4], I32)
        picked_s1 = tile("picked_s1", [P, J // 4], I32)
        nc.vector.memset(r8s_raw[:], 0)
        nc.vector.memset(w4s_raw[:], 0)
        nc.gpsimd.memset(tabs_raw[:], 0)
        nc.vector.memset(picked_s1[:], 0)

        def load(name, src):
            raw = tile(name, list(src.shape), src.dtype)
            nc.sync.dma_start(raw[:], src)
            return raw

        x_rows = x.rearrange("(a p t) m -> a p t m", a=2, t=PACK)
        wv_rows = wv.rearrange("(a p t) n -> a p t n", a=2, t=PACK)

        def load_x(q, a):
            return load("x_raw_%d_%d" % (q, a), x_rows[a, :, :, QUARTER * q : QUARTER * (q + 1)])

        def load_w4(a):
            return load("w4_raw_%d" % a, w4_words[a].bitcast(I32))

        def load_r8(a, b):
            words = r8_words[a].rearrange("p r i -> p (r i)").bitcast(I32)
            return load("r8_raw_%d_%d" % (a, b), words[:, PASS * b : PASS * (b + 1)])

        def quadrant_rows(scales, quad):
            return scales.bitcast(I32)[:, SCALE_ROWS * quad : SCALE_ROWS * (quad + 1), :]

        def load_stacked_scales(queue, raw, scales):
            for quad in range(P // QUADRANT):
                queue.dma_start(raw[QUADRANT * quad : QUADRANT * quad + 2 * SCALE_ROWS, :], quadrant_rows(scales, quad))

        x_raw, r8_raw, w4_raw = {}, {}, {}
        load_stacked_scales(nc.gpsimd, tabs_raw, tab_scales)
        x_raw[0, 0] = load_x(0, 0)
        r8_raw[0, 0] = load_r8(0, 0)
        load_stacked_scales(nc.sync, r8s_raw, r8_scales)
        r8_raw[0, 1] = load_r8(0, 1)
        w4_raw[0] = load_w4(0)
        for quad in range(P // QUADRANT):
            nc.sync.dma_start(
                w4s_raw[QUADRANT * quad : QUADRANT * quad + SCALE_ROWS, :].rearrange("p (a r) -> p a r", a=2),
                quadrant_rows(w4_scales, quad).rearrange("a row r -> row a r"),
            )
        x_raw[0, 1] = load_x(0, 1)
        r8_raw[1, 0] = load_r8(1, 0)
        r8_raw[1, 1] = load_r8(1, 1)
        w4_raw[1] = load_w4(1)
        x_raw[1, 0] = load_x(1, 0)
        x_raw[1, 1] = load_x(1, 1)
        x_raw[2, 0] = load_x(2, 0)
        offsets = keep.tile([P, J // 16], U16, name="offsets")
        nc.sync.dma_start(offsets[:], offs)
        x_raw[2, 1] = load_x(2, 1)
        tab_raw = load("tab_raw", tab_words[0].rearrange("p t i -> p (t i)").bitcast(I32))

        xq, qa = {}, {}
        w4 = [tile("w4_%d" % a, [P, 2 * R], U8) for a in range(2)]
        w4s = [tile("w4s_%d" % a, [P, R], U8) for a in range(2)]
        r8 = {(a, b): tile("r8_%d_%d" % (a, b), [P, PASS], I32) for a in range(2) for b in range(2)}
        r8s = [tile("r8s_%d" % b, [P, PASS], U8) for b in range(2)]

        def quantise_x(q, a, engines):
            xq[q, a] = weave_and_quantise("x_%d_%d" % (q, a), x_raw[q, a], engines)

        def order_w4(a):
            deal(w4[a][:].bitcast(U16), w4_raw[a][:].bitcast(U16), PACK, LINE // 2)

        def order_w4_scales(a):
            deal(w4s[a][:], w4s_raw[:].bitcast(U8)[:, R * a : R * (a + 1)], PACK, LINE)

        def order_r8(a, b):
            deal(r8[a, b][:], r8_raw[a, b][:], PACK, LINE // 4)

        def order_r8_scales(b):
            deal(r8s[b][:], r8s_raw[:].bitcast(U8)[:, PASS * b : PASS * (b + 1)], PACK, LINE)

        def query_pass(out, tier, q, a, b, t, cols, start, stop):
            if tier == "w4":
                c0 = 2 * P * t + P * b
                words, scales = w4[a][:, 2 * c0 : 2 * (c0 + P)].bitcast(FP4X4), w4s[a][:, c0 : c0 + P]
            else:
                words = r8[a, b][:, P * t : P * (t + 1)].bitcast(FP8X4)
                scales = r8s[b][SCALE_ROWS * a :, P * t : P * (t + 1)]
            codes, code_scales = xq[q, a]
            nc.tensor.matmul_mx(
                out=out,
                lhsT=words,
                lhsT_scale=scales,
                rhs=codes[:, cols].bitcast(FP8X4),
                rhs_scale=code_scales[:, cols],
                start=start,
                stop=stop,
            )

        def tier_passes(acc, tier, i, a, b, start=False, stop=False):
            cols = slice(P * (i % 2), P * (i % 2 + 1))
            for t in range(PACK):
                out = acc[:, P * t : P * (t + 1)]
                query_pass(out, tier, i // 2, a, b, t, cols, start and t == 0, stop and t == PACK - 1)

        qa_woven = [tile("qa_%d_woven" % i, [P, 2 * P, PACK], BF16) for i in range(M // P)]

        def empty_bank(acc, i, b):
            copy(SCALAR, qa_woven[i][:, P * b : P * (b + 1), :], acc[:].rearrange("p (t m) -> p m t", t=PACK))

        def quantise_qa(i):
            codes, scales = quantise("qa_%d" % i, qa_woven[i][:])
            qa[i] = [(codes[:, P * b : P * (b + 1)], scales[:, P * b : P * (b + 1)]) for b in range(2)]

        def queries(i, side):
            for b in range(2):
                acc = bank(side)
                tier_passes(acc, "r8", i, 0, b, start=True)
                tier_passes(acc, "w4", i, 0, b)
                tier_passes(acc, "r8", i, 1, b)
                tier_passes(acc, "w4", i, 1, b, stop=True)
                empty_bank(acc, i, b)
            quantise_qa(i)

        picked_s0 = tile("picked_s0", [P, J], U8)
        table = [tile("table_%d" % g, [P, 2 * 2 * BANK], U8) for g in range(2)]

        def listed(window, g):
            return window.indirect(offsets[:, BANK // 16 * g : BANK // 16 * (g + 1)])

        def gather_words(g):
            picked = tile("picked_%d" % g, [P, BANK], U32)
            nc.vector.tensor_copy(picked[:], listed(tab_raw[:].bitcast(U32), g))
            deal(table[g][:].bitcast(U16), picked[:].bitcast(U16), 2, LINE // 2)

        def relu_scaled(engine, out, in_):
            if engine == SCALAR:
                nc.scalar.activation(out, in_, ACT.Relu, scale=SCORE_SCALE)
            else:
                nc.vector.tensor_scalar(out, in_, 0.0, SCORE_SCALE, ALU.max, ALU.mult)

        def table_rows(name, stationary, leave, rows, split):
            staged = tile(name, [P, J], F32)
            for g, engine in enumerate((SCALAR, VECTOR)):
                cols = slice(BANK * g, BANK * (g + 1))
                acc = bank(1)
                for a, scale_bytes in enumerate((picked_s0[:], picked_s1[:].bitcast(U8))):
                    nc.tensor.matmul_mx(
                        out=acc[:],
                        lhsT=stationary[a][0].bitcast(FP8X4),
                        lhsT_scale=stationary[a][1],
                        rhs=table[g][:, 2 * BANK * a : 2 * BANK * (a + 1)].bitcast(FP4X4),
                        rhs_scale=scale_bytes[:, cols],
                        start=(a == 0),
                        stop=(a == 1),
                    )
                leave(engine, staged[:, cols], acc[:])
                if split:
                    nc.sync.dma_start(rows[:, cols], staged[:, cols])
            if not split:
                nc.sync.dma_start(rows, staged[:])

        def scores(i, split=False):
            table_rows("scores_%d" % i, qa[i], relu_scaled, out_0[P * i : P * (i + 1), :], split)

        def values(i, split=False):
            cols = slice(P * i, P * (i + 1))
            stationary = [(codes[:, cols], scales[:, cols]) for codes, scales in wvq]
            table_rows("values_%d" % i, stationary, copy, out_1[cols, :], split)

        order_r8(0, 0)
        quantise_x(0, 0, (SCALAR, VECTOR))
        order_r8_scales(0)
        order_r8_scales(1)
        order_r8(0, 1)
        order_w4(0)
        order_w4_scales(0)
        first = {(i, b): bank(0) for b in range(2) for i in range(2)}
        for tier in ("r8", "w4"):
            for i, b in first:
                tier_passes(first[i, b], tier, i, 0, b, start=(tier == "r8"))
        quantise_x(0, 1, (SCALAR, VECTOR))
        order_w4_scales(1)
        order_r8(1, 0)
        order_r8(1, 1)
        order_w4(1)
        for i, b in first:
            tier_passes(first[i, b], "r8", i, 1, b)
        for i, b in first:
            tier_passes(first[i, b], "w4", i, 1, b, stop=True)
            empty_bank(first[i, b], i, b)

        quantise_x(1, 0, (VECTOR,))
        quantise_x(1, 1, (VECTOR,))
        quantise_qa(0)
        quantise_qa(1)
        queries(2, 1)
        queries(3, 1)

        for g in range(2):
            nc.vector.tensor_copy(picked_s0[:, BANK * g : BANK * (g + 1)], listed(tabs_raw[:].bitcast(U8), g))
        for p0, rows in ((0, 64), (64, 32), (96, 4)):
            stacked = picked_s0[:].bitcast(I32)[p0 + SCALE_ROWS : p0 + SCALE_ROWS + rows, :]
            nc.sync.dma_start(picked_s1[p0 : p0 + rows, :], stacked)
        x_raw[3, 0] = load_x(3, 0)
        x_raw[3, 1] = load_x(3, 1)
        wv_raw = [load("wv_raw_%d" % a, wv_rows[a]) for a in range(2)]

        quantise_x(2, 0, (SCALAR,))
        quantise_x(2, 1, (SCALAR,))
        queries(4, 0)
        queries(5, 0)
        gather_words(0)
        gather_words(1)
        quantise_x(3, 0, (SCALAR,))
        quantise_x(3, 1, (SCALAR,))

        for i in range(4):
            scores(i)
        queries(6, 0)
        wvq = [weave_and_quantise("wv_%d" % a, wv_raw[a], (VECTOR,)) for a in range(2)]
        scores(4)
        scores(5)
        values(0)
        values(1)
        scores(6)
        queries(7, 0)
        values(2, split=True)
        values(3, split=True)
        scores(7, split=True)
